import numpy as np, ml_dtypes
CORES = [24,25,26,27,28,29,30,31]
N = 8
BF = ml_dtypes.bfloat16
def f(rng, *shape):
    return (rng.standard_normal(shape, dtype=np.float32) * np.exp2(rng.integers(-2, 3, shape[:-1] + (1,)))).astype(BF)
def wide(rng, *shape):
    v = f(rng, *shape).astype(np.float32); k = shape[:-2] + (1, shape[-1])
    return (v * np.exp2(rng.integers(-6, 7, k)) * (rng.random(k) > 0.0625)).astype(BF)
def gentries(a):
    return np.ascontiguousarray(a.reshape(8, 16, -1).transpose(0, 2, 1)).reshape(8, -1)
def gtable(e):
    e = np.asarray(e); return np.ascontiguousarray(e.reshape(8, -1, 16).transpose(0, 2, 1)).reshape(128, -1).astype(np.int32)
Q, CAPP, M, E, D = 256, 48, 2048, 4096, 4
LV, L = [1, 11, 130, 1000], 2000
EMPTY = 2 ** 24 - 1
def cut(rng, n, m, cap, s):
    u = rng.random((m, cap - 1)) + s * rng.random((m, 1))
    return 1 + np.bincount(np.argsort(u.reshape(-1))[:n - m] // (cap - 1), minlength=m)
def tree(rng, lv, n, keys, repeat=False):
    nk = np.sort(rng.integers(0, EMPTY - 16, (16, M)), axis=0) + np.arange(16)[:, None]
    nk[np.arange(16)[:, None] >= rng.integers(1, 17, (1, M))] = EMPTY
    beg = rng.integers(0, E - 15, M); kid = rng.integers(0, M, E)
    ids = np.concatenate([[0], 1 + rng.permutation(M - 1)]); a = np.cumsum([0] + list(lv))
    lev = [ids[a[l]:a[l + 1]] for l in range(D)]; nxt = lev[1:] + [rng.integers(0, M, n) if repeat else rng.permutation(M)[:n]]
    ek = np.asarray(keys); sizes = []
    for l in range(D - 1, -1, -1):
        sz = cut(rng, len(ek), lv[l], 16, 2.0); st = np.cumsum(sz) - sz
        nk[:, lev[l]] = EMPTY; nk[np.arange(len(ek)) - np.repeat(st, sz), np.repeat(lev[l], sz)] = ek
        ek = ek[st]; sizes.insert(0, sz)
    S = np.concatenate(sizes); C = np.concatenate(nxt); t = len(C); m = len(S)
    o = rng.permutation(m); so = S[o]; st = np.zeros(m, np.int64)
    st[o] = np.cumsum(so) - so + np.sort(rng.integers(0, E - 16 - t + 1, m))
    beg[ids[:m]] = st; kid[np.repeat(st - (np.cumsum(S) - S), S) + np.arange(t)] = C
    return nk, beg, kid
def make(rng, shapes=None, ends=False, full=False, alike=False, repeat=False):
    shapes = shapes or [(LV, L)] * N; I = np.int32
    spl = np.sort(rng.integers(0, EMPTY - 16384 * N + 1, (8, N - 1)), axis=1) + 16384 * np.arange(1, N)
    spl = np.concatenate([np.zeros((8, 1), np.int64), spl], axis=1); hi = np.concatenate([spl[:, 1:], np.full((8, 1), EMPTY)], axis=1)
    nk = np.zeros((N, 128, M), I); beg = np.zeros((N, 8, M), I); kid = np.zeros((N, 8, E), I); sk = np.zeros((N, 8, M), np.int64); ln = np.array([n for _, n in shapes])
    for r in range(N):
        lv, n = shapes[r]
        for g in range(8):
            w = int(hi[g, r] - spl[g, r])
            if ends: k = np.arange(n) + (w - n) * (r % 2)
            else: k = np.sort(rng.integers(0, w - n + 1, n)) + np.arange(n)
            k[0] = 0; k = k + spl[g, r]; sk[r, g, :n] = k
            nk[r, 16 * g:16 * g + 16], beg[r, g], kid[r, g] = tree(rng, lv, n, k, repeat)
    q = np.zeros((N, 8, Q), np.int64)
    for r in range(N):
        for g in range(8):
            if full: cn = np.zeros(N, np.int64); cn[rng.permutation(N)] = np.clip(Q - CAPP * np.arange(N), 0, CAPP)
            else: cn = 3 + cut(rng, Q - 3 * N, N, CAPP - 3, 0.5)
            own = np.repeat(np.arange(N), cn); st = np.cumsum(cn) - cn; occ = np.arange(Q) - st[own]
            a = spl[g, own]; b = hi[g, own]; k = sk[own, g, np.floor(rng.random(Q) * ln[own]).astype(np.int64)]
            inside = a + np.floor(rng.random(Q) * (b - a)).astype(np.int64)
            kd = 1 + occ % 4 if ends else np.array([0, 0, 0, 0, 0, 1, 1, 1, 2, 2, 2, 3, 4])[rng.integers(0, 13, Q)]
            v = np.choose(kd, [inside, k, np.maximum(k - 1, a), a, b - 1])
            if alike: v = v[st[own]]
            q[r, g] = v[rng.permutation(Q)]
    return {"nk": nk, "beg": beg, "kid": kid, "vec": f(rng, N, 128, M), "spl": np.stack([spl.astype(I)] * N), "q": np.stack([gtable(x) for x in q])}
def setup_inputs(rng):
    return make(rng)
def setup_inputs_caps(rng):
    return make(rng, full=True)
def setup_inputs_ends(rng):
    return make(rng, ends=True)
def setup_inputs_shapes(rng):
    a = []; n = M
    for l in range(D): n = -(-n // 16); a.insert(0, n)
    k = M * 3 // 8; b = [min(16 ** l, k) for l in range(D)]; s = int(rng.integers(0, 2))
    return make(rng, shapes=[(a, M) if (r + s) % 2 else (b, k) for r in range(N)], repeat=True)
def setup_inputs_alike(rng):
    return make(rng, alike=True)
def setup_inputs_spread(rng):
    d = make(rng); d["vec"] = wide(rng, N, 128, M); return d
def check_inputs(d):
    bad = []; nk, beg, kid, spl, q = [np.asarray(d[x]).astype(np.int64) for x in ("nk", "beg", "kid", "spl", "q")]
    if not np.isfinite(np.asarray(d["vec"]).astype(np.float32)).all(): bad.append("finite")
    if any(bool((a < 0).any() or (a > b).any()) for a, b in ((nk, EMPTY), (beg, E - 16), (kid, M - 1), (spl, EMPTY - 1), (q, EMPTY - 1))): return bad + ["ranges"]
    if (spl != spl[:1]).any() or (spl[:, :, 0] != 0).any() or (np.diff(spl, axis=2) <= 0).any(): return bad + ["splitters"]
    n4 = nk.reshape(N, 8, 16, M)
    if ((n4[:, :, 1:] <= n4[:, :, :-1]) & (n4[:, :, 1:] < EMPTY)).any(): bad.append("nodes")
    ok = True
    for r in range(N):
        for g in range(8):
            nd = np.zeros(1, np.int64); ek = spl[r, g, r:r + 1]; seen = [nd]
            for l in range(D):
                k = n4[r, g][:, nd].T
                if len(nd) > M or (k[:, 0] != ek).any(): ok = False; break
                use = k < EMPTY; ek = k[use]; nd = kid[r, g][(beg[r, g][nd][:, None] + np.arange(16))[use]]
                if l < D - 1:
                    seen.append(nd)
                    if len(nd) > M: ok = False; break
            if not ok: break
            s = np.concatenate(seen); top = spl[r, g, r + 1] if r + 1 < N else EMPTY
            if len(np.unique(s)) != len(s) or (np.diff(ek) <= 0).any() or ek[-1] >= top: ok = False
        if not ok: break
    if not ok: bad.append("tree")
    for r in range(N):
        x = gentries(q[r]); own = np.sum(x[:, :, None] >= spl[r][:, None, :], axis=2) - 1
        if any(np.bincount(own[g], minlength=N).max() > CAPP for g in range(8)): bad.append("caps"); break
    return bad
def reference(nk, beg, kid, vec, spl, q):
    y = np.zeros((N, 128, Q), vec.dtype); G = np.arange(8)[:, None]
    n4 = nk.reshape(N, 8, 16, M); v4 = vec.reshape(N, 8, 16, M)
    for r in range(N):
        x = gentries(q[r])
        own = np.sum(x[:, :, None] >= spl[r][:, None, :], axis=2) - 1
        at = np.zeros((8, Q), np.int64)
        for l in range(D):
            c = np.sum(n4[own, G, :, at] <= x[:, :, None], axis=2)
            at = kid[own, G, beg[own, G, at] + c - 1]
        y[r] = v4[own, G, :, at].transpose(0, 2, 1).reshape(128, Q)
    return {"y": y}

@@ -1,0 +1,245 @@
+from concourse.bass import DstId, RemoteDMATransfer
+from concourse.mybir import dt, AluOpType, ActivationFunctionType
+
+N, Q, CAP, M, E, D = 8, 256, 48, 2048, 4096, 4
+S = N * CAP
+H = S // 2
+OWN = S - CAP
+KW = E - 15
+BIG = 2 ** 24
+
+SCRATCH = {
+    "qrep": ("sbuf", [128, Q], "int32"),
+    "spc": ("sbuf", [128, 1], "int32"),
+    "lof": ("sbuf", [128, 1], "float32"),
+    "kp": ("sbuf", [128, 1], "int32"),
+    "kq": ("sbuf", [128, 1], "int32"),
+    "basec": ("sbuf", [128, 1], "float32"),
+    "ones": ("sbuf", [128, Q], "bfloat16"),
+    "idn": ("sbuf", [128, 128], "bfloat16"),
+    "sup": ("sbuf", [128, 128], "bfloat16"),
+    "sub": ("sbuf", [128, 128], "bfloat16"),
+    "eg0": ("sbuf", [128, 8], "bfloat16"),
+    "eg": ("sbuf", [128, 8], "bfloat16"),
+    "bz": ("sbuf", [128, 144], "bfloat16"),
+    "bsel": ("sbuf", [128, 144], "float16"),
+    "dm": ("sbuf", [128, 128], "float16"),
+    "em": ("sbuf", [128, 128], "float16"),
+    "ge": ("sbuf", [128, Q], "float16"),
+    "pos": ("sbuf", [128, Q], "float16"),
+    "w": ("sbuf", [128, Q], "float16"),
+    "off1": ("sbuf", [128, 16], "uint16"),
+    "off2": ("sbuf", [128, 16], "uint16"),
+    "z": ("sbuf", [128, S + OWN], "int32"),
+    "kids": ("sbuf", [128, KW], "int32"),
+    "bt": ("sbuf", [128, 128], "int32"),
+    "boff": ("sbuf", [128, 128], "uint16"),
+    "ct": ("sbuf", [128, M], "float16"),
+    "dwin": ("sbuf", [128, M], "float32"),
+    "nk0": ("sbuf", [128, 8], "int32"),
+    "key0": ("sbuf", [128, 1], "float32"),
+    "nkw": ("sbuf", [128, M], "int32"),
+    "vw": ("sbuf", [128, M], "bfloat16"),
+    "cmp": ("sbuf", [128, D * S], "float16"),
+    "pr": ("sbuf", [128, D * S], "float16"),
+    "offs": ("sbuf", [128, D * 32], "uint16"),
+    "yb": ("sbuf", [128, S + OWN], "bfloat16"),
+    "ysb": ("sbuf", [128, Q], "bfloat16"),
+    "psD": ("psum", [128, M], "float32"),
+    "psM": ("psum", [128, 512], "float32"),
+    "psL": ("psum", [128, 512], "float32"),
+    "psA": ("psum", [128, 512], "float32"),
+    "psB": ("psum", [128, 512], "float32"),
+}
+SEMAPHORES = ["e%d" % i for i in range(100)] + ["qin", "splin", "kidin", "arrA", "arrB", "retA", "retB", "sent"]
+
+
+def rank_program(g, core, T, topo):
+    me = T.rank_of(core)
+    if me is None:
+        return
+    A = AluOpType
+    V, P, S_, SY = g.vector, g.tensor, g.scalar, g.sync
+    COPY = ActivationFunctionType.Copy
+    cnt = [0]
+
+    def ev():
+        cnt[0] += 1
+        return T.sem["e%d" % (cnt[0] - 1)]
+
+    def do(instr, n=1):
+        e = ev()
+        instr.then_inc(e, n)
+        return (e, n)
+
+    def wait(q, *events):
+        for e, n in events:
+            q.wait_ge(e, n)
+
+    e_spc = do(V.memset(T.spc[:], BIG))
+    for o in range(8):
+        SY.dma_start(T.qrep[o::16, :], T.q[:]).then_inc(T.sem.qin, 16)
+        S_.dma_start(T.qrep[o + 8::16, :], T.q[:]).then_inc(T.sem.qin, 16)
+    wait(SY, e_spc)
+    wait(S_, e_spc)
+    for x in range(8):
+        (SY if x < 4 else S_).dma_start(T.spc[16 * x:16 * x + 8, 0:1], T.spl[x, :]).then_inc(T.sem.splin, 16)
+    e_bt = do(S_.dma_start(T.bt[:], T.beg[:]), 16)
+    for o in range(8):
+        SY.dma_start(T.kids[o::16, :], T.kid[:, o:o + KW]).then_inc(T.sem.kidin, 16)
+        S_.dma_start(T.kids[o + 8::16, :], T.kid[:, o + 8:o + 8 + KW]).then_inc(T.sem.kidin, 16)
+    e_nk0 = do(SY.dma_start(T.nk0[:], T.nk[:, 0:8]), 16)
+    q_in, spl_in, kid_in = (T.sem.qin, 256), (T.sem.splin, 128), (T.sem.kidin, 256)
+
+    e_ones = do(V.memset(T.ones[:], 1.0))
+    e_z0 = do(V.memset(T.z[:, 0:S], 0))
+    e_bz = do(V.memset(T.bz[:], 0.0))
+    wait(g, e_ones)
+    e_kp = do(g.iota(T.kp[:], [[0, 1]], 128 - me - 1, 1))
+    e_idn = do(g.affine_select(T.idn[:], T.ones[:, 0:128], [[-1, 128]], A.is_equal, 0.0, 0, 1))
+    e_sub = do(g.affine_select(T.sub[:], T.ones[:, 0:128], [[-1, 128]], A.is_equal, 0.0, -1, 1))
+    e_eg0 = do(g.affine_select(T.eg0[:], T.ones[:, 0:8], [[-16, 8]], A.is_ge, 0.0, 0, 1))
+    wait(g, e_eg0)
+    e_eg = do(g.affine_select(T.eg[:], T.eg0[:], [[16, 8]], A.is_ge, 0.0, 15, -1))
+    e_sup = do(g.affine_select(T.sup[:], T.ones[:, 0:128], [[-1, 128]], A.is_equal, 0.0, 1, 1))
+    wait(V, e_kp)
+    e = do(V.tensor_scalar(out=T.kq[:], in0=T.kp[:], scalar1=7, scalar2=None, op0=A.bitwise_and))
+    wait(V, e)
+    e_base = do(V.tensor_scalar(out=T.basec[:], in0=T.kq[:], scalar1=float(CAP), scalar2=-1.0, op0=A.mult, op1=A.add))
+    wait(V, e_sub)
+    e = do(V.memset(T.sub[:, 15::16], 0.0))
+    wait(V, e, e_idn)
+    e_em = do(V.tensor_tensor(out=T.em[:], in0=T.idn[:], in1=T.sub[:], op=A.subtract))
+    wait(V, e_eg, e_bz)
+    e = do(V.tensor_copy(out=T.bz[:, 15:143:16], in_=T.eg[:]))
+    wait(V, e)
+    e_bsel = do(V.tensor_copy(out=T.bsel[:], in_=T.bz[:]))
+    wait(V, e_sup)
+    e = do(V.memset(T.sup[:, 0::16], 0.0))
+    wait(V, e)
+    e_dm = do(V.tensor_tensor(out=T.dm[:], in0=T.idn[:], in1=T.sup[:], op=A.subtract))
+
+    def to_list(ps, cols):
+        for i in range(16):
+            m = P.matmul(ps, T.bsel[:, 15 - i:143 - i], cols(i), i == 0, i == 15)
+        return do(m)
+
+    wait(V, spl_in)
+    e = do(V.tensor_copy(out=T.lof[:], in_=T.spc[:]))
+    wait(V, e, q_in)
+    e_ge = do(V.tensor_scalar(out=T.ge[:], in0=T.qrep[:], scalar1=T.lof[:], scalar2=None, op0=A.is_ge))
+    wait(P, e_em, e_ge)
+    e_mask = do(P.matmul(T.psM[:, 0:Q], T.em[:], T.ge[:], True, True))
+    wait(V, e_mask, e_base)
+    e = do(V.tensor_tensor_scan(T.pos[:], T.ones[:], T.psM[:, 0:Q], T.basec[:], A.mult, A.add))
+    wait(V, e)
+    e_w = do(V.tensor_tensor(out=T.w[:], in0=T.psM[:, 0:Q], in1=T.pos[:], op=A.mult))
+    wait(P, e_w, e_bsel)
+    e_l1 = to_list(T.psL[:, 0:16], lambda i: T.w[:, i::16])
+    wait(V, e_l1)
+    e_off1 = do(V.tensor_copy(out=T.off1[:], in_=T.psL[:, 0:16]))
+    wait(V, e_off1, e_z0)
+    e_sc = do(V.tensor_copy(out=T.z[:, 0:S].indirect(T.off1[:, 0:16]), in_=T.qrep[:]))
+    wait(P, e_off1)
+    e_l2 = to_list(T.psL[:, 16:32], lambda i: T.w[:, 16 * i:16 * i + 16])
+
+    def transfer(buf, src_col, dst_col, peer, n, slot, sem):
+        dst = T.cores[peer]
+        rid, pid, _ = topo.addr(dst)
+        en = topo.engines(core, dst)[n * slot:n * slot + n]
+        return RemoteDMATransfer(dst_ids=[DstId(rid=rid, pnc=pid)], dma_engine_mask=sum(1 << x for x in en), remote_sem=sem,
+                                 src=buf[:, src_col:src_col + CAP], dst=buf[:, dst_col:dst_col + CAP])
+
+    wait(g, e_sc)
+    for ks, sem in (((6, 5, 4), T.sem.arrA), ((3, 2, 1, 0), T.sem.arrB)):
+        g.remote_dma_fused([transfer(T.z, CAP * k, S + CAP * (6 - k), (me + 1 + k) % N, 4, j, sem) for j, k in enumerate(ks)],
+                           local_sem=T.sem.sent)
+    e_go = ev()
+    g.sem_inc(e_go, 1)
+    wait(SY, (e_go, 1))
+    e_nk = do(SY.dma_start(T.nkw[:], T.nk[:]), 16)
+    e_vec = do(SY.dma_start(T.vw[:], T.vec[:]), 16)
+
+    wait(V, e_bt)
+    e = do(V.tensor_copy(out=T.boff[:], in_=T.bt[:]))
+    wait(V, e_nk0)
+    e_k0 = do(V.tensor_copy(out=T.key0[:], in_=T.nk0[:, 0:1]))
+    wait(V, e_l2)
+    e_off2 = do(V.tensor_copy(out=T.off2[:], in_=T.psL[:, 16:32]))
+    wait(V, e, kid_in)
+    e_ct = do(V.tensor_copy(out=T.ct[:], in_=T.kids[:].indirect(T.boff[:])))
+    wait(P, e_ct, e_dm)
+    e_d = []
+    for b in range(4):
+        for i in range(4 * b, 4 * b + 4):
+            m = P.matmul(T.psD[:, 128 * i:128 * i + 128], T.dm[:], T.ct[:, i::16], True, True)
+        e_p = do(m)
+        c = slice(512 * b, 512 * b + 512)
+        if b == 0:
+            wait(V, e_p)
+            e_d.append(do(V.tensor_copy(out=T.dwin[:, c], in_=T.psD[:, c])))
+        else:
+            wait(S_, e_p)
+            e_d.append(do(S_.activation(T.dwin[:, c], T.psD[:, c], COPY)))
+
+    X = (T.z[:, OWN:OWN + H], T.z[:, OWN + H:OWN + S])
+    ps = (T.psA, T.psB)
+    arr = ((T.sem.arrA, 12), (T.sem.arrB, 16))
+
+    def col(buf, l, h):
+        return buf[:, S * l + H * h:S * l + H * h + H]
+
+    def spread(l, h, e_pr):
+        wait(P, e_pr)
+        b = S * l + H * h
+        return to_list(ps[h][:, 16 * l:16 * l + 12], lambda i: T.pr[:, b + i:b + H:16])
+
+    lst = [None, None]
+    wait(V, e_k0, e_d[0])
+    for h in range(2):
+        wait(V, arr[h])
+        e_pr = do(V.tensor_scalar(out=col(T.pr, 0, h), in0=X[h], scalar1=T.key0[:], scalar2=T.dwin[:, 0:1], op0=A.is_ge, op1=A.mult))
+        lst[h] = spread(0, h, e_pr)
+    offs = [None, None]
+    for l in range(1, D + 1):
+        for h in range(2):
+            o = T.offs[:, 32 * (l - 1) + 16 * h:32 * (l - 1) + 16 * h + 12]
+            wait(V, lst[h])
+            e_o = do(V.tensor_copy(out=o, in_=ps[h][:, 16 * (l - 1):16 * (l - 1) + 12]))
+            if l < D:
+                wait(V, e_o)
+                if l == 1 and h == 0:
+                    wait(V, e_nk)
+                e_c = do(V.tensor_tensor(out=col(T.cmp, l, h), in0=T.nkw[:].indirect(o), in1=X[h], op=A.is_le))
+                wait(V, e_c)
+                if l == 1 and h == 0:
+                    wait(V, *e_d[1:])
+                e_pr = do(V.tensor_tensor(out=col(T.pr, l, h), in0=T.dwin[:].indirect(o), in1=col(T.cmp, l, h), op=A.mult))
+                lst[h] = spread(l, h, e_pr)
+            else:
+                out = T.yb[:, OWN + H * h:OWN + H * h + H]
+                if h == 0:
+                    wait(S_, e_o, e_vec)
+                    e_y = do(S_.activation(out, T.vw[:].indirect(o), COPY))
+                else:
+                    wait(V, e_o, e_vec)
+                    e_y = do(V.tensor_copy(out=out, in_=T.vw[:].indirect(o)))
+                wait(g, e_y)
+                sem = (T.sem.retA, T.sem.retB)[h]
+                g.remote_dma_fused([transfer(T.yb, S + CAP * k, CAP * (6 - k), (me + 1 + k) % N, 4, j, sem)
+                                    for j, k in enumerate(((0, 1, 2), (3, 4, 5, 6))[h])], local_sem=T.sem.sent)
+                offs[h] = e_y
+
+    for j, (q, dq) in enumerate(((V, SY), (S_, S_))):
+        wait(q, *offs)
+        wait(q, (T.sem.retA, 12), (T.sem.retB, 16), e_off2)
+        c = slice(128 * j, 128 * j + 128)
+        src = T.yb[:, 0:S].indirect(T.off2[:, 8 * j:8 * j + 8])
+        if j == 0:
+            e = do(V.tensor_copy(out=T.ysb[:, c], in_=src))
+        else:
+            e = do(S_.activation(T.ysb[:, c], src, COPY))
+        wait(dq, e)
+        e = do(dq.dma_start(T.y[:, c], T.ysb[:, c]), 16)
+        wait(dq, e)
+    g.wait_ge(T.sem.sent, 56)

@@ -7,6 +7,7 @@ H = S // 2
 OWN = S - CAP
 KW = E - 15
 BIG = 2 ** 24
+VC = 64
 
 SCRATCH = {
     "qrep": ("sbuf", [128, Q], "int32"),
@@ -36,6 +37,7 @@ SCRATCH = {
     "boff": ("sbuf", [128, 128], "uint16"),
     "ct": ("sbuf", [128, M], "float16"),
     "dwin": ("sbuf", [128, M], "float32"),
+    "d0": ("sbuf", [128, 1], "float32"),
     "nk0": ("sbuf", [128, 8], "int32"),
     "key0": ("sbuf", [128, 1], "float32"),
     "nkw": ("sbuf", [128, M], "int32"),
@@ -84,11 +86,13 @@ def rank_program(g, core, T, topo):
     wait(S_, e_spc)
     for x in range(8):
         (SY if x < 4 else S_).dma_start(T.spc[16 * x:16 * x + 8, 0:1], T.spl[x, :]).then_inc(T.sem.splin, 16)
-    e_bt = do(S_.dma_start(T.bt[:], T.beg[:]), 16)
     for o in range(8):
         SY.dma_start(T.kids[o::16, :], T.kid[:, o:o + KW]).then_inc(T.sem.kidin, 16)
         S_.dma_start(T.kids[o + 8::16, :], T.kid[:, o + 8:o + 8 + KW]).then_inc(T.sem.kidin, 16)
-    e_nk0 = do(SY.dma_start(T.nk0[:], T.nk[:, 0:8]), 16)
+        if o == 0:
+            e_bt = do(S_.dma_start(T.bt[:], T.beg[:]), 16)
+            e_nk0 = do(SY.dma_start(T.nk0[:], T.nk[:, 0:8]), 16)
+    e_nk = do(SY.dma_start(T.nkw[:], T.nk[:]), 16)
     q_in, spl_in, kid_in = (T.sem.qin, 256), (T.sem.splin, 128), (T.sem.kidin, 256)
 
     e_ones = do(V.memset(T.ones[:], 1.0))
@@ -157,30 +161,31 @@ def rank_program(g, core, T, topo):
     e_go = ev()
     g.sem_inc(e_go, 1)
     wait(SY, (e_go, 1))
-    e_nk = do(SY.dma_start(T.nkw[:], T.nk[:]), 16)
     e_vec = do(SY.dma_start(T.vw[:], T.vec[:]), 16)
 
     wait(V, e_bt)
-    e = do(V.tensor_copy(out=T.boff[:], in_=T.bt[:]))
+    e_bo = do(V.tensor_copy(out=T.boff[:], in_=T.bt[:]))
     wait(V, e_nk0)
     e_k0 = do(V.tensor_copy(out=T.key0[:], in_=T.nk0[:, 0:1]))
-    wait(V, e_l2)
-    e_off2 = do(V.tensor_copy(out=T.off2[:], in_=T.psL[:, 16:32]))
-    wait(V, e, kid_in)
-    e_ct = do(V.tensor_copy(out=T.ct[:], in_=T.kids[:].indirect(T.boff[:])))
+    wait(V, e_bo, kid_in)
+    e_ct = do(V.tensor_copy(out=T.ct[:, 0:16 * VC], in_=T.kids[:].indirect(T.boff[:, 0:VC])))
+    wait(S_, e_bo, kid_in)
+    e_cs = do(S_.activation(T.ct[:, 16 * VC:M], T.kids[:].indirect(T.boff[:, VC:128]), COPY))
     wait(P, e_ct, e_dm)
-    e_d = []
+    e_p0 = do(P.matmul(T.psM[:, 256:257], T.dm[:], T.ct[:, 0:1], True, True))
+    wait(V, e_p0)
+    e_d0 = do(V.tensor_copy(out=T.d0[:], in_=T.psM[:, 256:257]))
+    wait(P, e_cs)
+    e_p = []
     for b in range(4):
         for i in range(4 * b, 4 * b + 4):
             m = P.matmul(T.psD[:, 128 * i:128 * i + 128], T.dm[:], T.ct[:, i::16], True, True)
-        e_p = do(m)
+        e_p.append(do(m))
+    e_d = []
+    for b in range(1, 4):
         c = slice(512 * b, 512 * b + 512)
-        if b == 0:
-            wait(V, e_p)
-            e_d.append(do(V.tensor_copy(out=T.dwin[:, c], in_=T.psD[:, c])))
-        else:
-            wait(S_, e_p)
-            e_d.append(do(S_.activation(T.dwin[:, c], T.psD[:, c], COPY)))
+        wait(S_, e_p[b])
+        e_d.append(do(S_.activation(T.dwin[:, c], T.psD[:, c], COPY)))
 
     X = (T.z[:, OWN:OWN + H], T.z[:, OWN + H:OWN + S])
     ps = (T.psA, T.psB)
@@ -195,11 +200,13 @@ def rank_program(g, core, T, topo):
         return to_list(ps[h][:, 16 * l:16 * l + 12], lambda i: T.pr[:, b + i:b + H:16])
 
     lst = [None, None]
-    wait(V, e_k0, e_d[0])
+    wait(V, e_k0, e_d0)
     for h in range(2):
         wait(V, arr[h])
-        e_pr = do(V.tensor_scalar(out=col(T.pr, 0, h), in0=X[h], scalar1=T.key0[:], scalar2=T.dwin[:, 0:1], op0=A.is_ge, op1=A.mult))
+        e_pr = do(V.tensor_scalar(out=col(T.pr, 0, h), in0=X[h], scalar1=T.key0[:], scalar2=T.d0[:], op0=A.is_ge, op1=A.mult))
         lst[h] = spread(0, h, e_pr)
+    wait(V, e_p[0])
+    e_d.append(do(V.tensor_copy(out=T.dwin[:, 0:512], in_=T.psD[:, 0:512])))
     offs = [None, None]
     for l in range(1, D + 1):
         for h in range(2):
@@ -213,7 +220,7 @@ def rank_program(g, core, T, topo):
                 e_c = do(V.tensor_tensor(out=col(T.cmp, l, h), in0=T.nkw[:].indirect(o), in1=X[h], op=A.is_le))
                 wait(V, e_c)
                 if l == 1 and h == 0:
-                    wait(V, *e_d[1:])
+                    wait(V, *e_d)
                 e_pr = do(V.tensor_tensor(out=col(T.pr, l, h), in0=T.dwin[:].indirect(o), in1=col(T.cmp, l, h), op=A.mult))
                 lst[h] = spread(l, h, e_pr)
             else:
@@ -230,6 +237,8 @@ def rank_program(g, core, T, topo):
                                     for j, k in enumerate(((0, 1, 2), (3, 4, 5, 6))[h])], local_sem=T.sem.sent)
                 offs[h] = e_y
 
+    wait(V, e_l2)
+    e_off2 = do(V.tensor_copy(out=T.off2[:], in_=T.psL[:, 16:32]))
     for j, (q, dq) in enumerate(((V, SY), (S_, S_))):
         wait(q, *offs)
         wait(q, (T.sem.retA, 12), (T.sem.retB, 16), e_off2)

@@ -7,7 +7,8 @@ H = S // 2
 OWN = S - CAP
 KW = E - 15
 BIG = 2 ** 24
-VC = 64
+VC = 48
+NA = 1344
 
 SCRATCH = {
     "qrep": ("sbuf", [128, Q], "int32"),
@@ -34,26 +35,30 @@ SCRATCH = {
     "z": ("sbuf", [128, S + OWN], "int32"),
     "kids": ("sbuf", [128, KW], "int32"),
     "bt": ("sbuf", [128, 128], "int32"),
+    "bx": ("sbuf", [128, 128], "float32"),
+    "by": ("sbuf", [128, 128], "float32"),
     "boff": ("sbuf", [128, 128], "uint16"),
-    "ct": ("sbuf", [128, M], "float16"),
-    "dwin": ("sbuf", [128, M], "float32"),
+    "cz": ("sbuf", [128, 32], "float16"),
+    "ct": ("sbuf", [128, M], "float32"),
     "d0": ("sbuf", [128, 1], "float32"),
     "nk0": ("sbuf", [128, 8], "int32"),
     "key0": ("sbuf", [128, 1], "float32"),
     "nkw": ("sbuf", [128, M], "int32"),
     "vw": ("sbuf", [128, M], "bfloat16"),
     "cmp": ("sbuf", [128, D * S], "float16"),
+    "cg": ("sbuf", [128, D * S], "float16"),
     "pr": ("sbuf", [128, D * S], "float16"),
     "offs": ("sbuf", [128, D * 32], "uint16"),
     "yb": ("sbuf", [128, S + OWN], "bfloat16"),
     "ysb": ("sbuf", [128, Q], "bfloat16"),
-    "psD": ("psum", [128, M], "float32"),
     "psM": ("psum", [128, 512], "float32"),
     "psL": ("psum", [128, 512], "float32"),
     "psA": ("psum", [128, 512], "float32"),
     "psB": ("psum", [128, 512], "float32"),
+    "psP": ("psum", [128, 512], "float32"),
+    "psQ": ("psum", [128, 512], "float32"),
 }
-SEMAPHORES = ["e%d" % i for i in range(100)] + ["qin", "splin", "kidin", "arrA", "arrB", "retA", "retB", "sent"]
+SEMAPHORES = ["e%d" % i for i in range(120)] + ["qin", "splin", "kidin", "btin", "nkin", "arrA", "arrB", "retA", "retB", "sent"]
 
 
 def rank_program(g, core, T, topo):
@@ -78,7 +83,13 @@ def rank_program(g, core, T, topo):
         for e, n in events:
             q.wait_ge(e, n)
 
+    def kid_load(q, o):
+        q.dma_start(T.kids[o::16, :], T.kid[:, o:o + KW]).then_inc(T.sem.kidin, 16)
+
     e_spc = do(V.memset(T.spc[:], BIG))
+    kid_load(SY, 0)
+    for h in range(2):
+        S_.dma_start(T.bt[:, 64 * h:64 * h + 64], T.beg[h::2, :]).then_inc(T.sem.btin, 16)
     for o in range(8):
         SY.dma_start(T.qrep[o::16, :], T.q[:]).then_inc(T.sem.qin, 16)
         S_.dma_start(T.qrep[o + 8::16, :], T.q[:]).then_inc(T.sem.qin, 16)
@@ -86,47 +97,42 @@ def rank_program(g, core, T, topo):
     wait(S_, e_spc)
     for x in range(8):
         (SY if x < 4 else S_).dma_start(T.spc[16 * x:16 * x + 8, 0:1], T.spl[x, :]).then_inc(T.sem.splin, 16)
-    for o in range(8):
-        SY.dma_start(T.kids[o::16, :], T.kid[:, o:o + KW]).then_inc(T.sem.kidin, 16)
-        S_.dma_start(T.kids[o + 8::16, :], T.kid[:, o + 8:o + 8 + KW]).then_inc(T.sem.kidin, 16)
-        if o == 0:
-            e_bt = do(S_.dma_start(T.bt[:], T.beg[:]), 16)
-            e_nk0 = do(SY.dma_start(T.nk0[:], T.nk[:, 0:8]), 16)
-    e_nk = do(SY.dma_start(T.nkw[:], T.nk[:]), 16)
-    q_in, spl_in, kid_in = (T.sem.qin, 256), (T.sem.splin, 128), (T.sem.kidin, 256)
+    e_nk0 = do(SY.dma_start(T.nk0[:], T.nk[:, 0:8]), 16)
+    for o in range(1, 16):
+        kid_load(S_ if o % 2 and o < 15 else SY, o)
+    SY.dma_start(T.nkw[:, 0:NA], T.nk[:, 0:NA]).then_inc(T.sem.nkin, 16)
+    q_in, spl_in, kid_in, bt_in, nk_in = (T.sem.qin, 256), (T.sem.splin, 128), (T.sem.kidin, 256), (T.sem.btin, 32), (T.sem.nkin, 32)
 
     e_ones = do(V.memset(T.ones[:], 1.0))
-    e_z0 = do(V.memset(T.z[:, 0:S], 0))
     e_bz = do(V.memset(T.bz[:], 0.0))
+    e_z0 = do(V.memset(T.z[:, 0:S], 0))
     wait(g, e_ones)
-    e_kp = do(g.iota(T.kp[:], [[0, 1]], 128 - me - 1, 1))
     e_idn = do(g.affine_select(T.idn[:], T.ones[:, 0:128], [[-1, 128]], A.is_equal, 0.0, 0, 1))
     e_sub = do(g.affine_select(T.sub[:], T.ones[:, 0:128], [[-1, 128]], A.is_equal, 0.0, -1, 1))
+    e_kp = do(g.iota(T.kp[:], [[0, 1]], 128 - me - 1, 1))
     e_eg0 = do(g.affine_select(T.eg0[:], T.ones[:, 0:8], [[-16, 8]], A.is_ge, 0.0, 0, 1))
     wait(g, e_eg0)
     e_eg = do(g.affine_select(T.eg[:], T.eg0[:], [[16, 8]], A.is_ge, 0.0, 15, -1))
     e_sup = do(g.affine_select(T.sup[:], T.ones[:, 0:128], [[-1, 128]], A.is_equal, 0.0, 1, 1))
-    wait(V, e_kp)
-    e = do(V.tensor_scalar(out=T.kq[:], in0=T.kp[:], scalar1=7, scalar2=None, op0=A.bitwise_and))
-    wait(V, e)
-    e_base = do(V.tensor_scalar(out=T.basec[:], in0=T.kq[:], scalar1=float(CAP), scalar2=-1.0, op0=A.mult, op1=A.add))
     wait(V, e_sub)
     e = do(V.memset(T.sub[:, 15::16], 0.0))
     wait(V, e, e_idn)
     e_em = do(V.tensor_tensor(out=T.em[:], in0=T.idn[:], in1=T.sub[:], op=A.subtract))
-    wait(V, e_eg, e_bz)
-    e = do(V.tensor_copy(out=T.bz[:, 15:143:16], in_=T.eg[:]))
+    wait(V, e_kp)
+    e = do(V.tensor_scalar(out=T.kq[:], in0=T.kp[:], scalar1=7, scalar2=None, op0=A.bitwise_and))
     wait(V, e)
-    e_bsel = do(V.tensor_copy(out=T.bsel[:], in_=T.bz[:]))
-    wait(V, e_sup)
-    e = do(V.memset(T.sup[:, 0::16], 0.0))
-    wait(V, e)
-    e_dm = do(V.tensor_tensor(out=T.dm[:], in0=T.idn[:], in1=T.sup[:], op=A.subtract))
+    e_base = do(V.tensor_scalar(out=T.basec[:], in0=T.kq[:], scalar1=float(CAP), scalar2=-1.0, op0=A.mult, op1=A.add))
 
     def to_list(ps, cols):
         for i in range(16):
             m = P.matmul(ps, T.bsel[:, 15 - i:143 - i], cols(i), i == 0, i == 15)
         return do(m)
+
+    wait(S_, bt_in)
+    e_bx = []
+    for h in range(2):
+        for b in range(4):
+            e_bx.append(do(S_.activation(T.bx[:, 32 * b + 16 * h:32 * b + 16 * h + 16], T.bt[:, 64 * h + 16 * b:64 * h + 16 * b + 16], COPY)))
 
     wait(V, spl_in)
     e = do(V.tensor_copy(out=T.lof[:], in_=T.spc[:]))
@@ -134,18 +140,26 @@ def rank_program(g, core, T, topo):
     e_ge = do(V.tensor_scalar(out=T.ge[:], in0=T.qrep[:], scalar1=T.lof[:], scalar2=None, op0=A.is_ge))
     wait(P, e_em, e_ge)
     e_mask = do(P.matmul(T.psM[:, 0:Q], T.em[:], T.ge[:], True, True))
+    wait(V, e_eg, e_bz)
+    e = do(V.tensor_copy(out=T.bz[:, 15:143:16], in_=T.eg[:]))
+    wait(V, e)
+    e_bsel = do(V.tensor_copy(out=T.bsel[:], in_=T.bz[:]))
     wait(V, e_mask, e_base)
     e = do(V.tensor_tensor_scan(T.pos[:], T.ones[:], T.psM[:, 0:Q], T.basec[:], A.mult, A.add))
     wait(V, e)
     e_w = do(V.tensor_tensor(out=T.w[:], in0=T.psM[:, 0:Q], in1=T.pos[:], op=A.mult))
     wait(P, e_w, e_bsel)
     e_l1 = to_list(T.psL[:, 0:16], lambda i: T.w[:, i::16])
+    wait(V, *e_bx)
+    e_by = do(V.transpose(T.by[:], T.bx[:]))
     wait(V, e_l1)
     e_off1 = do(V.tensor_copy(out=T.off1[:], in_=T.psL[:, 0:16]))
     wait(V, e_off1, e_z0)
     e_sc = do(V.tensor_copy(out=T.z[:, 0:S].indirect(T.off1[:, 0:16]), in_=T.qrep[:]))
     wait(P, e_off1)
     e_l2 = to_list(T.psL[:, 16:32], lambda i: T.w[:, 16 * i:16 * i + 16])
+    wait(S_, e_by)
+    e_bo = [do(S_.activation(T.boff[:, b::4], T.by[:, 32 * b:32 * b + 32], COPY)) for b in range(4)]
 
     def transfer(buf, src_col, dst_col, peer, n, slot, sem):
         dst = T.cores[peer]
@@ -161,34 +175,30 @@ def rank_program(g, core, T, topo):
     e_go = ev()
     g.sem_inc(e_go, 1)
     wait(SY, (e_go, 1))
+    SY.dma_start(T.nkw[:, NA:M], T.nk[:, NA:M]).then_inc(T.sem.nkin, 16)
     e_vec = do(SY.dma_start(T.vw[:], T.vec[:]), 16)
 
-    wait(V, e_bt)
-    e_bo = do(V.tensor_copy(out=T.boff[:], in_=T.bt[:]))
+    wait(V, e_sup)
+    e = do(V.memset(T.sup[:, 0::16], 0.0))
+    wait(V, e)
+    e_dm = do(V.tensor_tensor(out=T.dm[:], in0=T.idn[:], in1=T.sup[:], op=A.subtract))
     wait(V, e_nk0)
     e_k0 = do(V.tensor_copy(out=T.key0[:], in_=T.nk0[:, 0:1]))
-    wait(V, e_bo, kid_in)
+    wait(V, e_l2)
+    e_off2 = do(V.tensor_copy(out=T.off2[:], in_=T.psL[:, 16:32]))
+    wait(V, kid_in, *e_bo)
+    e_cz = do(V.tensor_copy(out=T.cz[:], in_=T.kids[:].indirect(T.boff[:, 0:2])))
     e_ct = do(V.tensor_copy(out=T.ct[:, 0:16 * VC], in_=T.kids[:].indirect(T.boff[:, 0:VC])))
-    wait(S_, e_bo, kid_in)
+    wait(S_, kid_in, *e_bo)
     e_cs = do(S_.activation(T.ct[:, 16 * VC:M], T.kids[:].indirect(T.boff[:, VC:128]), COPY))
-    wait(P, e_ct, e_dm)
-    e_p0 = do(P.matmul(T.psM[:, 256:257], T.dm[:], T.ct[:, 0:1], True, True))
+    wait(P, e_cz, e_dm)
+    e_p0 = do(P.matmul(T.psM[:, 256:257], T.dm[:], T.cz[:, 0:1], True, True))
     wait(V, e_p0)
     e_d0 = do(V.tensor_copy(out=T.d0[:], in_=T.psM[:, 256:257]))
-    wait(P, e_cs)
-    e_p = []
-    for b in range(4):
-        for i in range(4 * b, 4 * b + 4):
-            m = P.matmul(T.psD[:, 128 * i:128 * i + 128], T.dm[:], T.ct[:, i::16], True, True)
-        e_p.append(do(m))
-    e_d = []
-    for b in range(1, 4):
-        c = slice(512 * b, 512 * b + 512)
-        wait(S_, e_p[b])
-        e_d.append(do(S_.activation(T.dwin[:, c], T.psD[:, c], COPY)))
 
     X = (T.z[:, OWN:OWN + H], T.z[:, OWN + H:OWN + S])
     ps = (T.psA, T.psB)
+    po = (T.psP, T.psQ)
     arr = ((T.sem.arrA, 12), (T.sem.arrB, 16))
 
     def col(buf, l, h):
@@ -199,46 +209,56 @@ def rank_program(g, core, T, topo):
         b = S * l + H * h
         return to_list(ps[h][:, 16 * l:16 * l + 12], lambda i: T.pr[:, b + i:b + H:16])
 
+    def offsets(l, h):
+        o = T.offs[:, 32 * (l - 1) + 16 * h:32 * (l - 1) + 16 * h + 12]
+        wait(V, lst[h])
+        return o, do(V.tensor_copy(out=o, in_=ps[h][:, 16 * (l - 1):16 * (l - 1) + 12]))
+
+    def compare(l, h, o, e_o):
+        wait(S_, e_o)
+        if l == 1 and h == 0:
+            wait(S_, e_ct, e_cs)
+        e_g = do(S_.activation(col(T.cg, l, h), T.ct[:].indirect(o), COPY))
+        wait(V, e_o)
+        if l == 1 and h == 0:
+            wait(V, nk_in)
+        e_c = do(V.tensor_tensor(out=col(T.cmp, l, h), in0=T.nkw[:].indirect(o), in1=X[h], op=A.is_le))
+        wait(P, e_c)
+        return e_g, do(P.matmul(po[h][:, 0:H], T.em[:], col(T.cmp, l, h), True, True))
+
+    def pick(l, h, e_g, e_one):
+        wait(V, e_g, e_one)
+        return do(V.tensor_tensor(out=col(T.pr, l, h), in0=po[h][:, 0:H], in1=col(T.cg, l, h), op=A.mult))
+
     lst = [None, None]
     wait(V, e_k0, e_d0)
     for h in range(2):
         wait(V, arr[h])
         e_pr = do(V.tensor_scalar(out=col(T.pr, 0, h), in0=X[h], scalar1=T.key0[:], scalar2=T.d0[:], op0=A.is_ge, op1=A.mult))
         lst[h] = spread(0, h, e_pr)
-    wait(V, e_p[0])
-    e_d.append(do(V.tensor_copy(out=T.dwin[:, 0:512], in_=T.psD[:, 0:512])))
-    offs = [None, None]
-    for l in range(1, D + 1):
+    for l in range(1, D):
+        es = [compare(l, h, *offsets(l, h)) for h in range(2)]
         for h in range(2):
-            o = T.offs[:, 32 * (l - 1) + 16 * h:32 * (l - 1) + 16 * h + 12]
-            wait(V, lst[h])
-            e_o = do(V.tensor_copy(out=o, in_=ps[h][:, 16 * (l - 1):16 * (l - 1) + 12]))
-            if l < D:
-                wait(V, e_o)
-                if l == 1 and h == 0:
-                    wait(V, e_nk)
-                e_c = do(V.tensor_tensor(out=col(T.cmp, l, h), in0=T.nkw[:].indirect(o), in1=X[h], op=A.is_le))
-                wait(V, e_c)
-                if l == 1 and h == 0:
-                    wait(V, *e_d)
-                e_pr = do(V.tensor_tensor(out=col(T.pr, l, h), in0=T.dwin[:].indirect(o), in1=col(T.cmp, l, h), op=A.mult))
-                lst[h] = spread(l, h, e_pr)
-            else:
-                out = T.yb[:, OWN + H * h:OWN + H * h + H]
-                if h == 0:
-                    wait(S_, e_o, e_vec)
-                    e_y = do(S_.activation(out, T.vw[:].indirect(o), COPY))
-                else:
-                    wait(V, e_o, e_vec)
-                    e_y = do(V.tensor_copy(out=out, in_=T.vw[:].indirect(o)))
-                wait(g, e_y)
-                sem = (T.sem.retA, T.sem.retB)[h]
-                g.remote_dma_fused([transfer(T.yb, S + CAP * k, CAP * (6 - k), (me + 1 + k) % N, 4, j, sem)
-                                    for j, k in enumerate(((0, 1, 2), (3, 4, 5, 6))[h])], local_sem=T.sem.sent)
-                offs[h] = e_y
+            lst[h] = spread(l, h, pick(l, h, *es[h]))
+    offs = []
+    for h in range(2):
+        o, e_o = offsets(D, h)
+        out = OWN + H * h
+        if h == 0:
+            wait(S_, e_o, e_vec)
+            e_y = [do(S_.activation(T.yb[:, out:out + H], T.vw[:].indirect(o), COPY))]
+        else:
+            b = 32 * (D - 1) + 16 * h
+            wait(S_, e_o, e_vec)
+            e_y = [do(S_.activation(T.yb[:, out + H // 2:out + H], T.vw[:].indirect(T.offs[:, b + 6:b + 12]), COPY))]
+            wait(V, e_o, e_vec)
+            e_y.append(do(V.tensor_copy(out=T.yb[:, out:out + H // 2], in_=T.vw[:].indirect(T.offs[:, b:b + 6]))))
+        wait(g, *e_y)
+        sem = (T.sem.retA, T.sem.retB)[h]
+        g.remote_dma_fused([transfer(T.yb, S + CAP * k, CAP * (6 - k), (me + 1 + k) % N, 4, j, sem)
+                            for j, k in enumerate(((0, 1, 2), (3, 4, 5, 6))[h])], local_sem=T.sem.sent)
+        offs += e_y
 
-    wait(V, e_l2)
-    e_off2 = do(V.tensor_copy(out=T.off2[:], in_=T.psL[:, 16:32]))
     for j, (q, dq) in enumerate(((V, SY), (S_, S_))):
         wait(q, *offs)
         wait(q, (T.sem.retA, 12), (T.sem.retB, 16), e_off2)

from concourse.bass import DstId, RemoteDMATransfer
from concourse.mybir import dt, AluOpType, ActivationFunctionType

N, Q, CAP, M, E, D = 8, 256, 48, 2048, 4096, 4
S = N * CAP
H = S // 2
OWN = S - CAP
KW = E - 15
BIG = 2 ** 24
VC = 48
NA = 1344

SCRATCH = {
    "qrep": ("sbuf", [128, Q], "int32"),
    "spc": ("sbuf", [128, 1], "int32"),
    "lof": ("sbuf", [128, 1], "float32"),
    "kp": ("sbuf", [128, 1], "int32"),
    "kq": ("sbuf", [128, 1], "int32"),
    "basec": ("sbuf", [128, 1], "float32"),
    "ones": ("sbuf", [128, Q], "bfloat16"),
    "idn": ("sbuf", [128, 128], "bfloat16"),
    "sup": ("sbuf", [128, 128], "bfloat16"),
    "sub": ("sbuf", [128, 128], "bfloat16"),
    "eg0": ("sbuf", [128, 8], "bfloat16"),
    "eg": ("sbuf", [128, 8], "bfloat16"),
    "bz": ("sbuf", [128, 144], "bfloat16"),
    "bsel": ("sbuf", [128, 144], "float16"),
    "dm": ("sbuf", [128, 128], "float16"),
    "em": ("sbuf", [128, 128], "float16"),
    "ge": ("sbuf", [128, Q], "float16"),
    "pos": ("sbuf", [128, Q], "float16"),
    "w": ("sbuf", [128, Q], "float16"),
    "off1": ("sbuf", [128, 16], "uint16"),
    "off2": ("sbuf", [128, 16], "uint16"),
    "z": ("sbuf", [128, S + OWN], "int32"),
    "kids": ("sbuf", [128, KW], "int32"),
    "bt": ("sbuf", [128, 128], "int32"),
    "bx": ("sbuf", [128, 128], "float32"),
    "by": ("sbuf", [128, 128], "float32"),
    "boff": ("sbuf", [128, 128], "uint16"),
    "cz": ("sbuf", [128, 32], "float16"),
    "ct": ("sbuf", [128, M], "float32"),
    "d0": ("sbuf", [128, 1], "float32"),
    "nk0": ("sbuf", [128, 8], "int32"),
    "key0": ("sbuf", [128, 1], "float32"),
    "nkw": ("sbuf", [128, M], "int32"),
    "vw": ("sbuf", [128, M], "bfloat16"),
    "cmp": ("sbuf", [128, D * S], "float16"),
    "cg": ("sbuf", [128, D * S], "float16"),
    "pr": ("sbuf", [128, D * S], "float16"),
    "offs": ("sbuf", [128, D * 32], "uint16"),
    "yb": ("sbuf", [128, S + OWN], "bfloat16"),
    "ysb": ("sbuf", [128, Q], "bfloat16"),
    "psM": ("psum", [128, 512], "float32"),
    "psL": ("psum", [128, 512], "float32"),
    "psA": ("psum", [128, 512], "float32"),
    "psB": ("psum", [128, 512], "float32"),
    "psP": ("psum", [128, 512], "float32"),
    "psQ": ("psum", [128, 512], "float32"),
}
SEMAPHORES = ["e%d" % i for i in range(120)] + ["qin", "splin", "kidin", "btin", "nkin", "arrA", "arrB", "retA", "retB", "sent"]


def rank_program(g, core, T, topo):
    me = T.rank_of(core)
    if me is None:
        return
    A = AluOpType
    V, P, S_, SY = g.vector, g.tensor, g.scalar, g.sync
    COPY = ActivationFunctionType.Copy
    cnt = [0]

    def ev():
        cnt[0] += 1
        return T.sem["e%d" % (cnt[0] - 1)]

    def do(instr, n=1):
        e = ev()
        instr.then_inc(e, n)
        return (e, n)

    def wait(q, *events):
        for e, n in events:
            q.wait_ge(e, n)

    def kid_load(q, o):
        q.dma_start(T.kids[o::16, :], T.kid[:, o:o + KW]).then_inc(T.sem.kidin, 16)

    e_spc = do(V.memset(T.spc[:], BIG))
    kid_load(SY, 0)
    for h in range(2):
        S_.dma_start(T.bt[:, 64 * h:64 * h + 64], T.beg[h::2, :]).then_inc(T.sem.btin, 16)
    for o in range(8):
        SY.dma_start(T.qrep[o::16, :], T.q[:]).then_inc(T.sem.qin, 16)
        S_.dma_start(T.qrep[o + 8::16, :], T.q[:]).then_inc(T.sem.qin, 16)
    wait(SY, e_spc)
    wait(S_, e_spc)
    for x in range(8):
        (SY if x < 4 else S_).dma_start(T.spc[16 * x:16 * x + 8, 0:1], T.spl[x, :]).then_inc(T.sem.splin, 16)
    e_nk0 = do(SY.dma_start(T.nk0[:], T.nk[:, 0:8]), 16)
    for o in range(1, 16):
        kid_load(S_ if o % 2 and o < 15 else SY, o)
    SY.dma_start(T.nkw[:, 0:NA], T.nk[:, 0:NA]).then_inc(T.sem.nkin, 16)
    q_in, spl_in, kid_in, bt_in, nk_in = (T.sem.qin, 256), (T.sem.splin, 128), (T.sem.kidin, 256), (T.sem.btin, 32), (T.sem.nkin, 32)

    e_ones = do(V.memset(T.ones[:], 1.0))
    e_bz = do(V.memset(T.bz[:], 0.0))
    e_z0 = do(V.memset(T.z[:, 0:S], 0))
    wait(g, e_ones)
    e_idn = do(g.affine_select(T.idn[:], T.ones[:, 0:128], [[-1, 128]], A.is_equal, 0.0, 0, 1))
    e_sub = do(g.affine_select(T.sub[:], T.ones[:, 0:128], [[-1, 128]], A.is_equal, 0.0, -1, 1))
    e_kp = do(g.iota(T.kp[:], [[0, 1]], 128 - me - 1, 1))
    e_eg0 = do(g.affine_select(T.eg0[:], T.ones[:, 0:8], [[-16, 8]], A.is_ge, 0.0, 0, 1))
    wait(g, e_eg0)
    e_eg = do(g.affine_select(T.eg[:], T.eg0[:], [[16, 8]], A.is_ge, 0.0, 15, -1))
    e_sup = do(g.affine_select(T.sup[:], T.ones[:, 0:128], [[-1, 128]], A.is_equal, 0.0, 1, 1))
    wait(V, e_sub)
    e = do(V.memset(T.sub[:, 15::16], 0.0))
    wait(V, e, e_idn)
    e_em = do(V.tensor_tensor(out=T.em[:], in0=T.idn[:], in1=T.sub[:], op=A.subtract))
    wait(V, e_kp)
    e = do(V.tensor_scalar(out=T.kq[:], in0=T.kp[:], scalar1=7, scalar2=None, op0=A.bitwise_and))
    wait(V, e)
    e_base = do(V.tensor_scalar(out=T.basec[:], in0=T.kq[:], scalar1=float(CAP), scalar2=-1.0, op0=A.mult, op1=A.add))

    def to_list(ps, cols):
        for i in range(16):
            m = P.matmul(ps, T.bsel[:, 15 - i:143 - i], cols(i), i == 0, i == 15)
        return do(m)

    wait(S_, bt_in)
    e_bx = []
    for h in range(2):
        for b in range(4):
            e_bx.append(do(S_.activation(T.bx[:, 32 * b + 16 * h:32 * b + 16 * h + 16], T.bt[:, 64 * h + 16 * b:64 * h + 16 * b + 16], COPY)))

    wait(V, spl_in)
    e = do(V.tensor_copy(out=T.lof[:], in_=T.spc[:]))
    wait(V, e, q_in)
    e_ge = do(V.tensor_scalar(out=T.ge[:], in0=T.qrep[:], scalar1=T.lof[:], scalar2=None, op0=A.is_ge))
    wait(P, e_em, e_ge)
    e_mask = do(P.matmul(T.psM[:, 0:Q], T.em[:], T.ge[:], True, True))
    wait(V, e_eg, e_bz)
    e = do(V.tensor_copy(out=T.bz[:, 15:143:16], in_=T.eg[:]))
    wait(V, e)
    e_bsel = do(V.tensor_copy(out=T.bsel[:], in_=T.bz[:]))
    wait(V, e_mask, e_base)
    e = do(V.tensor_tensor_scan(T.pos[:], T.ones[:], T.psM[:, 0:Q], T.basec[:], A.mult, A.add))
    wait(V, e)
    e_w = do(V.tensor_tensor(out=T.w[:], in0=T.psM[:, 0:Q], in1=T.pos[:], op=A.mult))
    wait(P, e_w, e_bsel)
    e_l1 = to_list(T.psL[:, 0:16], lambda i: T.w[:, i::16])
    wait(V, *e_bx)
    e_by = do(V.transpose(T.by[:], T.bx[:]))
    wait(V, e_l1)
    e_off1 = do(V.tensor_copy(out=T.off1[:], in_=T.psL[:, 0:16]))
    wait(V, e_off1, e_z0)
    e_sc = do(V.tensor_copy(out=T.z[:, 0:S].indirect(T.off1[:, 0:16]), in_=T.qrep[:]))
    wait(P, e_off1)
    e_l2 = to_list(T.psL[:, 16:32], lambda i: T.w[:, 16 * i:16 * i + 16])
    wait(S_, e_by)
    e_bo = [do(S_.activation(T.boff[:, b::4], T.by[:, 32 * b:32 * b + 32], COPY)) for b in range(4)]

    def transfer(buf, src_col, dst_col, peer, n, slot, sem):
        dst = T.cores[peer]
        rid, pid, _ = topo.addr(dst)
        en = topo.engines(core, dst)[n * slot:n * slot + n]
        return RemoteDMATransfer(dst_ids=[DstId(rid=rid, pnc=pid)], dma_engine_mask=sum(1 << x for x in en), remote_sem=sem,
                                 src=buf[:, src_col:src_col + CAP], dst=buf[:, dst_col:dst_col + CAP])

    wait(g, e_sc)
    for ks, sem in (((6, 5, 4), T.sem.arrA), ((3, 2, 1, 0), T.sem.arrB)):
        g.remote_dma_fused([transfer(T.z, CAP * k, S + CAP * (6 - k), (me + 1 + k) % N, 4, j, sem) for j, k in enumerate(ks)],
                           local_sem=T.sem.sent)
    e_go = ev()
    g.sem_inc(e_go, 1)
    wait(SY, (e_go, 1))
    SY.dma_start(T.nkw[:, NA:M], T.nk[:, NA:M]).then_inc(T.sem.nkin, 16)
    e_vec = do(SY.dma_start(T.vw[:], T.vec[:]), 16)

    wait(V, e_sup)
    e = do(V.memset(T.sup[:, 0::16], 0.0))
    wait(V, e)
    e_dm = do(V.tensor_tensor(out=T.dm[:], in0=T.idn[:], in1=T.sup[:], op=A.subtract))
    wait(V, e_nk0)
    e_k0 = do(V.tensor_copy(out=T.key0[:], in_=T.nk0[:, 0:1]))
    wait(V, e_l2)
    e_off2 = do(V.tensor_copy(out=T.off2[:], in_=T.psL[:, 16:32]))
    wait(V, kid_in, *e_bo)
    e_cz = do(V.tensor_copy(out=T.cz[:], in_=T.kids[:].indirect(T.boff[:, 0:2])))
    e_ct = do(V.tensor_copy(out=T.ct[:, 0:16 * VC], in_=T.kids[:].indirect(T.boff[:, 0:VC])))
    wait(S_, kid_in, *e_bo)
    e_cs = do(S_.activation(T.ct[:, 16 * VC:M], T.kids[:].indirect(T.boff[:, VC:128]), COPY))
    wait(P, e_cz, e_dm)
    e_p0 = do(P.matmul(T.psM[:, 256:257], T.dm[:], T.cz[:, 0:1], True, True))
    wait(V, e_p0)
    e_d0 = do(V.tensor_copy(out=T.d0[:], in_=T.psM[:, 256:257]))

    X = (T.z[:, OWN:OWN + H], T.z[:, OWN + H:OWN + S])
    ps = (T.psA, T.psB)
    po = (T.psP, T.psQ)
    arr = ((T.sem.arrA, 12), (T.sem.arrB, 16))

    def col(buf, l, h):
        return buf[:, S * l + H * h:S * l + H * h + H]

    def spread(l, h, e_pr):
        wait(P, e_pr)
        b = S * l + H * h
        return to_list(ps[h][:, 16 * l:16 * l + 12], lambda i: T.pr[:, b + i:b + H:16])

    def offsets(l, h):
        o = T.offs[:, 32 * (l - 1) + 16 * h:32 * (l - 1) + 16 * h + 12]
        wait(V, lst[h])
        return o, do(V.tensor_copy(out=o, in_=ps[h][:, 16 * (l - 1):16 * (l - 1) + 12]))

    def compare(l, h, o, e_o):
        wait(S_, e_o)
        if l == 1 and h == 0:
            wait(S_, e_ct, e_cs)
        e_g = do(S_.activation(col(T.cg, l, h), T.ct[:].indirect(o), COPY))
        wait(V, e_o)
        if l == 1 and h == 0:
            wait(V, nk_in)
        e_c = do(V.tensor_tensor(out=col(T.cmp, l, h), in0=T.nkw[:].indirect(o), in1=X[h], op=A.is_le))
        wait(P, e_c)
        return e_g, do(P.matmul(po[h][:, 0:H], T.em[:], col(T.cmp, l, h), True, True))

    def pick(l, h, e_g, e_one):
        wait(V, e_g, e_one)
        return do(V.tensor_tensor(out=col(T.pr, l, h), in0=po[h][:, 0:H], in1=col(T.cg, l, h), op=A.mult))

    lst = [None, None]
    wait(V, e_k0, e_d0)
    for h in range(2):
        wait(V, arr[h])
        e_pr = do(V.tensor_scalar(out=col(T.pr, 0, h), in0=X[h], scalar1=T.key0[:], scalar2=T.d0[:], op0=A.is_ge, op1=A.mult))
        lst[h] = spread(0, h, e_pr)
    for l in range(1, D):
        es = [compare(l, h, *offsets(l, h)) for h in range(2)]
        for h in range(2):
            lst[h] = spread(l, h, pick(l, h, *es[h]))
    offs = []
    for h in range(2):
        o, e_o = offsets(D, h)
        out = OWN + H * h
        if h == 0:
            wait(S_, e_o, e_vec)
            e_y = [do(S_.activation(T.yb[:, out:out + H], T.vw[:].indirect(o), COPY))]
        else:
            b = 32 * (D - 1) + 16 * h
            wait(S_, e_o, e_vec)
            e_y = [do(S_.activation(T.yb[:, out + H // 2:out + H], T.vw[:].indirect(T.offs[:, b + 6:b + 12]), COPY))]
            wait(V, e_o, e_vec)
            e_y.append(do(V.tensor_copy(out=T.yb[:, out:out + H // 2], in_=T.vw[:].indirect(T.offs[:, b:b + 6]))))
        wait(g, *e_y)
        sem = (T.sem.retA, T.sem.retB)[h]
        g.remote_dma_fused([transfer(T.yb, S + CAP * k, CAP * (6 - k), (me + 1 + k) % N, 4, j, sem)
                            for j, k in enumerate(((0, 1, 2), (3, 4, 5, 6))[h])], local_sem=T.sem.sent)
        offs += e_y

    for j, (q, dq) in enumerate(((V, SY), (S_, S_))):
        wait(q, *offs)
        wait(q, (T.sem.retA, 12), (T.sem.retB, 16), e_off2)
        c = slice(128 * j, 128 * j + 128)
        src = T.yb[:, 0:S].indirect(T.off2[:, 8 * j:8 * j + 8])
        if j == 0:
            e = do(V.tensor_copy(out=T.ysb[:, c], in_=src))
        else:
            e = do(S_.activation(T.ysb[:, c], src, COPY))
        wait(dq, e)
        e = do(dq.dma_start(T.y[:, c], T.ysb[:, c]), 16)
        wait(dq, e)
    g.wait_ge(T.sem.sent, 56)
